import numpy as np
import ml_dtypes


def mxq(x, axis, fmt="e4m3"):
    dtype, down = {"e4m3": (ml_dtypes.float8_e4m3fn, 7), "e5m2": (ml_dtypes.float8_e5m2, 14)}[fmt]
    v = np.moveaxis(np.asarray(x, np.float32).astype(ml_dtypes.bfloat16).astype(np.float64), axis, -1)
    blocks = v.reshape(v.shape[:-1] + (-1, 32))
    amax = np.abs(blocks).max(-1, keepdims=True)
    byte = np.maximum(np.where(amax > 0, np.frexp(amax)[1] - 1 + 127, 0) - down, 1)
    scale = np.exp2(byte - 127.0)
    codes = (blocks / scale).astype(np.float32).astype(dtype).astype(np.float64)
    return np.moveaxis((codes * scale).reshape(v.shape), -1, axis)


WIDE = False


def mx_kscale(k):
    if not WIDE:
        return np.ones(k)
    levels = np.array([10, -10, 5, -5, 0])
    if k % 512:
        return np.exp2(np.random.permutation(np.resize(levels, k // 32))).repeat(32)
    a = np.empty((k // 512, 16))
    for p in range(k // 512):
        a[p, :8] = np.random.permutation(np.resize(levels, 8))
        for g in range(8):
            far = levels[np.abs(levels - a[p, g]) >= 10]
            a[p, g + 8] = far[np.random.randint(len(far))]
    return np.exp2(a.ravel()).repeat(32)


def f64(x):
    return np.asarray(x).astype(np.float64)


def striped(idx):
    return np.tile(idx.reshape(-1, 16).T, (8, 1)).astype(np.uint16)


def unstriped(offs):
    return offs[:16].T.reshape(-1).astype(np.int64)


def pack_weight(w):
    k, n = w.shape
    w = f64(np.asarray(w, np.float32).astype(ml_dtypes.bfloat16)).reshape(k // 32, 32, n)
    amax = np.abs(w).max(1)
    byte = np.clip(np.where(amax > 0, np.frexp(amax)[1] - 1 + 127 - 7, 1), 1, 254)
    scaled = (w * np.exp2(127.0 - byte)[:, None, :]).reshape(k, n).astype(np.float32)
    words = np.ascontiguousarray(scaled.reshape(k // 512, 128, 4, n).transpose(0, 1, 3, 2)).astype(ml_dtypes.float8_e4m3fn).view(np.uint8)
    return words, np.ascontiguousarray(byte.astype(np.uint8).reshape(k // 512, 16, n))


def unpack_weight(words, scales):
    g, p, n, _ = words.shape
    vals = np.ascontiguousarray(words).view(ml_dtypes.float8_e4m3fn).astype(np.float64) * np.repeat(np.exp2(scales.astype(np.float64) - 127.0), 8, axis=1)[..., None]
    return vals.transpose(0, 1, 3, 2).reshape(g * 512, n)


def sigmoid(v):
    return 1.0 / (1.0 + np.exp(-np.maximum(v, -700.0)))


K, T, S, N = 512, 1024, 512, 256
P = 2 ** 7


def setup_inputs():
    n = np.random.standard_normal
    s = mx_kscale(K)[:, None]
    packed_xT = pack_weight(n((K, T)) * s)
    return {
        "x_words": packed_xT[0],
        "x_scales": packed_xT[1],
        "w1": (n((K, N)) / np.sqrt(K) / s).astype(np.float32),
        "w2": (n((K, N)) / np.sqrt(K) / s).astype(np.float32),
        "w3": (n((K, N)) / np.sqrt(K) / s).astype(np.float32),
        "logt": (n((N, S))).astype(np.float32),
        "seen": (np.tile((np.random.uniform(size=S) < 0.6) * 1.0, (P, 1))).astype(np.float32),
        "offs": striped(np.random.permutation(T)[:S]),
    }


def reference(x_words, x_scales, w1, w2, w3, logt, seen, offs):
    xq = unpack_weight(x_words, x_scales)[:, unstriped(offs)]
    yp = mxq(f64(w3), 0, "e4m3").T @ xq
    cure = 0.6 * sigmoid(yp)
    ym = mxq(f64(w1), 0, "e4m3").T @ xq
    ys = mxq(f64(w2), 0, "e4m3").T @ xq
    isg = np.log(np.exp(ys) + 1.0) + 0.4
    zs = 0.6 * ((f64(logt) - ym) * isg)
    surv = np.exp(-1.0 * np.exp(zs))
    return cure + (-1.0 * cure + 1.0) * surv - (f64(seen)[:1] * (np.exp(-1.0 * (zs * zs))))

@@ -1,0 +1,178 @@
+from contextlib import ExitStack
+
+import concourse.mybir as mybir
+
+K, T, S, N = 512, 1024, 512, 256
+FLOPS = 3 * 2 * K * N * S
+
+F32 = mybir.dt.float32
+BF16 = mybir.dt.bfloat16
+I32 = mybir.dt.int32
+U32 = mybir.dt.uint32
+U16 = mybir.dt.uint16
+U8 = mybir.dt.uint8
+FP8X4 = mybir.dt.float8_e4m3fn_x4
+ACT = mybir.ActivationFunctionType
+ALU = mybir.AluOpType
+
+P = 128
+PACK = 4
+MT = N // P
+HALVES = 2
+SH = S // HALVES
+W = MT * SH
+EPS = 2.0 ** -44
+
+
+def tile_picked_ywbaft_surv_p_kernel(tc, x_words, x_scales, w1, w2, w3, logt, seen, offs, out):
+    nc = tc.nc
+    with ExitStack() as ctx:
+        keep = ctx.enter_context(tc.tile_pool(name="keep", bufs=1))
+        psum = ctx.enter_context(tc.psum_pool(name="psum", bufs=1))
+
+        offsets = keep.tile([P, S // 16], U16, name="offsets")
+        nc.sync.dma_start(offsets[:], offs)
+
+        scale_table = keep.tile([P, T], U8, name="scale_table", align_bytes=64)
+        nc.vector.memset(scale_table[:].bitcast(I32), 0)
+        for quad in range(4):
+            nc.sync.dma_start(
+                scale_table[32 * quad : 32 * quad + 4, :].bitcast(I32),
+                x_scales[0, 4 * quad : 4 * quad + 4, :].bitcast(I32),
+            )
+
+        def rows_by_four(w):
+            return w.rearrange("(p j) n -> p j n", j=PACK)
+
+        w2_raw = keep.tile([P, PACK, N], F32, name="w2_raw", tag="staged")
+        nc.scalar.dma_start(w2_raw[:], rows_by_four(w2))
+        word_table = keep.tile([P, T], I32, name="word_table", align_bytes=64)
+        nc.scalar.dma_start(word_table[:], x_words[0].rearrange("p c t -> p (c t)").bitcast(I32))
+        w1_raw = keep.tile([P, PACK, N], F32, name="w1_raw")
+        nc.scalar.dma_start(w1_raw[:], rows_by_four(w1))
+
+        eps = keep.tile([P, 1], F32, name="eps")
+        nc.gpsimd.memset(eps[:], EPS)
+        warm = keep.tile([P, 1], F32, name="warm")
+        nc.scalar.activation(warm[:], eps[:], ACT.Sigmoid)
+
+        x_scale = keep.tile([P, S], U8, name="x_scale", align_bytes=64)
+        nc.vector.tensor_copy(x_scale[:], scale_table[:].indirect(offsets[:]))
+
+        def interleave(raw, name, engines):
+            grouped = keep.tile([P, N, PACK], BF16, name=name + "_bf", align_bytes=64)
+            for m in range(MT):
+                cols = slice(m * P, (m + 1) * P)
+                src = raw[:, :, cols].rearrange("p j (c i) -> p c j i", i=4)
+                dst = grouped[:, cols, :].rearrange("p (c i) j -> p c j i", i=4)
+                if engines[m] == "scalar":
+                    nc.scalar.copy(dst, src)
+                else:
+                    nc.vector.tensor_copy(dst, src)
+            return grouped
+
+        def quantize(grouped, name):
+            codes = keep.tile([P, N], U32, name=name + "_codes", align_bytes=64)
+            scales = keep.tile([P, N], U8, name=name + "_scales", align_bytes=64)
+            nc.vector.quantize_mx(
+                out=codes[:].bitcast(FP8X4), scales=scales[:], in_=grouped[:].rearrange("p n j -> p (n j)")
+            )
+            return codes, scales
+
+        x_code = []
+
+        def gather_words(h):
+            xc = keep.tile([P, SH], U32, name="x_code%d" % h, align_bytes=64)
+            cols = SH // 16
+            nc.vector.tensor_copy(xc[:], word_table[:].bitcast(U32).indirect(offsets[:, h * cols : (h + 1) * cols]))
+            x_code.append(xc)
+
+        def product(wq, h, name):
+            codes, scales = wq
+            bank = psum.tile([P, W], F32, name="%s%d" % (name, h))
+            for m in range(MT):
+                nc.tensor.matmul_mx(
+                    out=bank[:, m * SH : (m + 1) * SH],
+                    lhsT=codes[:, m * P : (m + 1) * P].bitcast(FP8X4),
+                    lhsT_scale=scales[:, m * P : (m + 1) * P],
+                    rhs=x_code[h][:].bitcast(FP8X4),
+                    rhs_scale=x_scale[:, h * SH : (h + 1) * SH],
+                    start=True,
+                    stop=True,
+                )
+            return bank
+
+        w2q = quantize(interleave(w2_raw, "w2", ("scalar", "vector")), "w2")
+        late = keep.tile([P, MT * S + PACK * N + S], F32, name="late", tag="staged")
+        logt_sb = late[:, : MT * S].rearrange("p (m s) -> p m s", m=MT)
+        w3_raw = late[:, MT * S : MT * S + PACK * N].rearrange("p (j n) -> p j n", j=PACK)
+        seen_sb = late[:, MT * S + PACK * N :]
+        nc.sync.dma_start(logt_sb, logt.rearrange("(m p) s -> p m s", p=P))
+        nc.sync.dma_start(w3_raw, rows_by_four(w3))
+        nc.sync.dma_start(seen_sb, seen)
+        sig = keep.tile([P, HALVES * W], F32, name="sig")
+        ys = []
+        for h in range(HALVES):
+            gather_words(h)
+            ys.append(product(w2q, h, "ys"))
+            nc.scalar.activation(sig[:, h * W : (h + 1) * W], ys[h][:], ACT.Sigmoid, scale=-1.0)
+
+        w1q = quantize(interleave(w1_raw, "w1", ("vector", "vector")), "w1")
+        ym = [product(w1q, h, "ym") for h in range(HALVES)]
+        diff = []
+        for h in range(HALVES):
+            d = keep.tile([P, W], F32, name="diff%d" % h)
+            nc.vector.tensor_tensor(
+                d[:].rearrange("p (m s) -> p m s", m=MT),
+                ym[h][:].rearrange("p (m s) -> p m s", m=MT),
+                logt_sb[:, :, h * SH : (h + 1) * SH],
+                ALU.subtract,
+            )
+            diff.append(d)
+        w3q = quantize(interleave(w3_raw, "w3", ("vector", "vector")), "w3")
+        yp = [product(w3q, h, "yp") for h in range(HALVES)]
+
+        lg = keep.tile([P, HALVES * W], F32, name="lg")
+        nc.scalar.activation(lg[:, : W + 8], sig[:, : W + 8], ACT.Ln, bias=eps[:])
+        nc.scalar.activation(lg[:, W + 8 :], sig[:, W + 8 :], ACT.Ln, bias=eps[:])
+
+        z = []
+        zsq = []
+        for h in range(HALVES):
+            neg = keep.tile([P, W], F32, name="neg%d" % h)
+            nc.vector.scalar_tensor_tensor(neg[:], ys[h][:], -1.0, lg[:, h * W : (h + 1) * W], ALU.mult, ALU.min)
+            zz = keep.tile([P, W], F32, name="z%d" % h)
+            nc.vector.scalar_tensor_tensor(zz[:], neg[:], 0.4, diff[h][:], ALU.subtract, ALU.mult)
+            z.append(zz)
+            q = keep.tile([P, W], F32, name="zsq%d" % h)
+            nc.vector.tensor_tensor(q[:], z[h][:], z[h][:], ALU.mult)
+            zsq.append(q)
+
+        for h in range(HALVES):
+            th = sig[:, (1 - h) * W : (2 - h) * W]
+            nc.scalar.activation(th, yp[h][:], ACT.Tanh, scale=0.5)
+            bump = keep.tile([P, W], F32, name="bump%d" % h)
+            nc.scalar.activation(bump[:], zsq[h][:], ACT.Exp, scale=-0.36)
+            ez = keep.tile([P, W], F32, name="ez%d" % h)
+            nc.scalar.activation(ez[:], z[h][:], ACT.Exp, scale=0.6)
+            surv = keep.tile([P, W], F32, name="surv%d" % h)
+            nc.scalar.activation(surv[:], ez[:], ACT.Exp, scale=-1.0)
+            alive = keep.tile([P, W], F32, name="alive%d" % h)
+            nc.vector.tensor_scalar(alive[:], th, -0.3, 0.7, ALU.mult, ALU.add)
+            hit = keep.tile([P, MT, SH], F32, name="hit%d" % h)
+            nc.vector.tensor_tensor(
+                hit[:],
+                bump[:].rearrange("p (m s) -> p m s", m=MT),
+                seen_sb[:, h * SH : (h + 1) * SH].unsqueeze(1).to_broadcast([P, MT, SH]),
+                ALU.mult,
+            )
+            lost = keep.tile([P, W], F32, name="lost%d" % h)
+            nc.vector.scalar_tensor_tensor(lost[:], surv[:], 1.0, alive[:], ALU.subtract, ALU.mult)
+            res = keep.tile([P, W], F32, name="res%d" % h)
+            nc.vector.scalar_tensor_tensor(
+                res[:], lost[:], 1.0, hit[:].rearrange("p m s -> p (m s)"), ALU.add, ALU.subtract
+            )
+            nc.sync.dma_start(
+                out[:, h * SH : (h + 1) * SH].rearrange("(m p) s -> p m s", p=P),
+                res[:].rearrange("p (m s) -> p m s", m=MT),
+            )

@@ -30,37 +30,38 @@ def tile_picked_ywbaft_surv_p_kernel(tc, x_words, x_scales, w1, w2, w3, logt, se
         keep = ctx.enter_context(tc.tile_pool(name="keep", bufs=1))
         psum = ctx.enter_context(tc.psum_pool(name="psum", bufs=1))
 
+        def rows_by_four(w):
+            return w.rearrange("(p j) n -> p j n", j=PACK)
+
         offsets = keep.tile([P, S // 16], U16, name="offsets")
         nc.sync.dma_start(offsets[:], offs)
-
-        scale_table = keep.tile([P, T], U8, name="scale_table", align_bytes=64)
+        scale_table = keep.tile([P, T], U8, name="scale_table", tag="w2_codes", align_bytes=64)
         nc.vector.memset(scale_table[:].bitcast(I32), 0)
+        w2_raw = keep.tile([P, PACK, N], F32, name="w2_raw")
+        nc.sync.dma_start(w2_raw[:], rows_by_four(w2))
         for quad in range(4):
             nc.sync.dma_start(
                 scale_table[32 * quad : 32 * quad + 4, :].bitcast(I32),
                 x_scales[0, 4 * quad : 4 * quad + 4, :].bitcast(I32),
             )
-
-        def rows_by_four(w):
-            return w.rearrange("(p j) n -> p j n", j=PACK)
-
-        w2_raw = keep.tile([P, PACK, N], F32, name="w2_raw", tag="staged")
-        nc.scalar.dma_start(w2_raw[:], rows_by_four(w2))
         word_table = keep.tile([P, T], I32, name="word_table", align_bytes=64)
-        nc.scalar.dma_start(word_table[:], x_words[0].rearrange("p c t -> p (c t)").bitcast(I32))
+        nc.sync.dma_start(word_table[:], x_words[0].rearrange("p c t -> p (c t)").bitcast(I32))
         w1_raw = keep.tile([P, PACK, N], F32, name="w1_raw")
-        nc.scalar.dma_start(w1_raw[:], rows_by_four(w1))
+        nc.sync.dma_start(w1_raw[:], rows_by_four(w1))
+        w3_raw = keep.tile([P, PACK, N], F32, name="w3_raw")
+        nc.sync.dma_start(w3_raw[:], rows_by_four(w3))
+        logt_sb = keep.tile([P, MT, S], F32, name="logt_sb")
+        nc.sync.dma_start(logt_sb[:], logt.rearrange("(m p) s -> p m s", p=P))
+        seen_sb = keep.tile([P, S], F32, name="seen_sb")
+        nc.sync.dma_start(seen_sb[:], seen)
 
         eps = keep.tile([P, 1], F32, name="eps")
         nc.gpsimd.memset(eps[:], EPS)
         warm = keep.tile([P, 1], F32, name="warm")
         nc.scalar.activation(warm[:], eps[:], ACT.Sigmoid)
 
-        x_scale = keep.tile([P, S], U8, name="x_scale", align_bytes=64)
-        nc.vector.tensor_copy(x_scale[:], scale_table[:].indirect(offsets[:]))
-
         def interleave(raw, name, engines):
-            grouped = keep.tile([P, N, PACK], BF16, name=name + "_bf", align_bytes=64)
+            grouped = keep.tile([P, N, PACK], BF16, name=name + "_bf", tag=name + "_bf", align_bytes=64)
             for m in range(MT):
                 cols = slice(m * P, (m + 1) * P)
                 src = raw[:, :, cols].rearrange("p j (c i) -> p c j i", i=4)
@@ -72,7 +73,7 @@ def tile_picked_ywbaft_surv_p_kernel(tc, x_words, x_scales, w1, w2, w3, logt, se
             return grouped
 
         def quantize(grouped, name):
-            codes = keep.tile([P, N], U32, name=name + "_codes", align_bytes=64)
+            codes = keep.tile([P, N], U32, name=name + "_codes", tag=name + "_codes", align_bytes=64)
             scales = keep.tile([P, N], U8, name=name + "_scales", align_bytes=64)
             nc.vector.quantize_mx(
                 out=codes[:].bitcast(FP8X4), scales=scales[:], in_=grouped[:].rearrange("p n j -> p (n j)")
@@ -80,12 +81,19 @@ def tile_picked_ywbaft_surv_p_kernel(tc, x_words, x_scales, w1, w2, w3, logt, se
             return codes, scales
 
         x_code = []
+        x_scale = []
 
         def gather_words(h):
-            xc = keep.tile([P, SH], U32, name="x_code%d" % h, align_bytes=64)
+            xc = keep.tile([P, SH], U32, name="x_code%d" % h, tag=("x_code0", "w2_bf")[h], align_bytes=64)
             cols = SH // 16
             nc.vector.tensor_copy(xc[:], word_table[:].bitcast(U32).indirect(offsets[:, h * cols : (h + 1) * cols]))
             x_code.append(xc)
+
+        def gather_scales(h):
+            xs = keep.tile([P, SH], U8, name="x_scale%d" % h, align_bytes=64)
+            cols = SH // 16
+            nc.vector.tensor_copy(xs[:], scale_table[:].indirect(offsets[:, h * cols : (h + 1) * cols]))
+            x_scale.append(xs)
 
         def product(wq, h, name):
             codes, scales = wq
@@ -96,22 +104,17 @@ def tile_picked_ywbaft_surv_p_kernel(tc, x_words, x_scales, w1, w2, w3, logt, se
                     lhsT=codes[:, m * P : (m + 1) * P].bitcast(FP8X4),
                     lhsT_scale=scales[:, m * P : (m + 1) * P],
                     rhs=x_code[h][:].bitcast(FP8X4),
-                    rhs_scale=x_scale[:, h * SH : (h + 1) * SH],
+                    rhs_scale=x_scale[h][:],
                     start=True,
                     stop=True,
                 )
             return bank
 
-        w2q = quantize(interleave(w2_raw, "w2", ("scalar", "vector")), "w2")
-        late = keep.tile([P, MT * S + PACK * N + S], F32, name="late", tag="staged")
-        logt_sb = late[:, : MT * S].rearrange("p (m s) -> p m s", m=MT)
-        w3_raw = late[:, MT * S : MT * S + PACK * N].rearrange("p (j n) -> p j n", j=PACK)
-        seen_sb = late[:, MT * S + PACK * N :]
-        nc.sync.dma_start(logt_sb, logt.rearrange("(m p) s -> p m s", p=P))
-        nc.sync.dma_start(w3_raw, rows_by_four(w3))
-        nc.sync.dma_start(seen_sb, seen)
         sig = keep.tile([P, HALVES * W], F32, name="sig")
         ys = []
+        for h in range(HALVES):
+            gather_scales(h)
+        w2q = quantize(interleave(w2_raw, "w2", ("scalar", "scalar")), "w2")
         for h in range(HALVES):
             gather_words(h)
             ys.append(product(w2q, h, "ys"))
@@ -119,6 +122,8 @@ def tile_picked_ywbaft_surv_p_kernel(tc, x_words, x_scales, w1, w2, w3, logt, se
 
         w1q = quantize(interleave(w1_raw, "w1", ("vector", "vector")), "w1")
         ym = [product(w1q, h, "ym") for h in range(HALVES)]
+        w3q = quantize(interleave(w3_raw, "w3", ("vector", "vector")), "w3")
+        yp = [product(w3q, h, "yp") for h in range(HALVES)]
         diff = []
         for h in range(HALVES):
             d = keep.tile([P, W], F32, name="diff%d" % h)
@@ -129,50 +134,92 @@ def tile_picked_ywbaft_surv_p_kernel(tc, x_words, x_scales, w1, w2, w3, logt, se
                 ALU.subtract,
             )
             diff.append(d)
-        w3q = quantize(interleave(w3_raw, "w3", ("vector", "vector")), "w3")
-        yp = [product(w3q, h, "yp") for h in range(HALVES)]
 
         lg = keep.tile([P, HALVES * W], F32, name="lg")
         nc.scalar.activation(lg[:, : W + 8], sig[:, : W + 8], ACT.Ln, bias=eps[:])
         nc.scalar.activation(lg[:, W + 8 :], sig[:, W + 8 :], ACT.Ln, bias=eps[:])
 
+        neg = []
+        for h in range(HALVES):
+            ng = keep.tile([P, W], F32, name="neg%d" % h, tag=("w3_bf", "w1_bf")[h], align_bytes=64)
+            nc.vector.scalar_tensor_tensor(ng[:], ys[h][:], -1.0, lg[:, h * W : (h + 1) * W], ALU.mult, ALU.min)
+            neg.append(ng)
         z = []
+        for h in range(HALVES):
+            zz = keep.tile([P, W], F32, name="z%d" % h)
+            nc.vector.scalar_tensor_tensor(zz[:], neg[h][:], 0.4, diff[h][:], ALU.subtract, ALU.mult)
+            z.append(zz)
         zsq = []
         for h in range(HALVES):
-            neg = keep.tile([P, W], F32, name="neg%d" % h)
-            nc.vector.scalar_tensor_tensor(neg[:], ys[h][:], -1.0, lg[:, h * W : (h + 1) * W], ALU.mult, ALU.min)
-            zz = keep.tile([P, W], F32, name="z%d" % h)
-            nc.vector.scalar_tensor_tensor(zz[:], neg[:], 0.4, diff[h][:], ALU.subtract, ALU.mult)
-            z.append(zz)
             q = keep.tile([P, W], F32, name="zsq%d" % h)
             nc.vector.tensor_tensor(q[:], z[h][:], z[h][:], ALU.mult)
             zsq.append(q)
+        th = [sig[:, (1 - h) * W : (2 - h) * W] for h in range(HALVES)]
+        bump = [keep.tile([P, W], F32, name="bump%d" % h) for h in range(HALVES)]
+        ez = [keep.tile([P, W], F32, name="ez%d" % h) for h in range(HALVES)]
+        surv = [keep.tile([P, W], F32, name="surv%d" % h) for h in range(HALVES)]
+        alive = [keep.tile([P, W], F32, name="alive%d" % h) for h in range(HALVES)]
+        hit = [keep.tile([P, W], F32, name="hit%d" % h) for h in range(HALVES)]
+        lost = [keep.tile([P, W], F32, name="lost%d" % h) for h in range(HALVES)]
+        res = [keep.tile([P, W], F32, name="res%d" % h) for h in range(HALVES)]
 
-        for h in range(HALVES):
-            th = sig[:, (1 - h) * W : (2 - h) * W]
-            nc.scalar.activation(th, yp[h][:], ACT.Tanh, scale=0.5)
-            bump = keep.tile([P, W], F32, name="bump%d" % h)
-            nc.scalar.activation(bump[:], zsq[h][:], ACT.Exp, scale=-0.36)
-            ez = keep.tile([P, W], F32, name="ez%d" % h)
-            nc.scalar.activation(ez[:], z[h][:], ACT.Exp, scale=0.6)
-            surv = keep.tile([P, W], F32, name="surv%d" % h)
-            nc.scalar.activation(surv[:], ez[:], ACT.Exp, scale=-1.0)
-            alive = keep.tile([P, W], F32, name="alive%d" % h)
-            nc.vector.tensor_scalar(alive[:], th, -0.3, 0.7, ALU.mult, ALU.add)
-            hit = keep.tile([P, MT, SH], F32, name="hit%d" % h)
+        def do_tanh(h):
+            nc.scalar.activation(th[h], yp[h][:], ACT.Tanh, scale=0.5)
+
+        def do_ez(h):
+            nc.scalar.activation(ez[h][:], z[h][:], ACT.Exp, scale=0.6)
+
+        def do_bump(h):
+            nc.scalar.activation(bump[h][:], zsq[h][:], ACT.Exp, scale=-0.36)
+
+        def do_surv(h, cols):
+            nc.scalar.activation(surv[h][:, cols], ez[h][:, cols], ACT.Exp, scale=-1.0)
+
+        def do_alive(h):
+            nc.vector.tensor_scalar(alive[h][:], th[h], -0.3, 0.7, ALU.mult, ALU.add)
+
+        def do_hit(h):
             nc.vector.tensor_tensor(
-                hit[:],
-                bump[:].rearrange("p (m s) -> p m s", m=MT),
+                hit[h][:].rearrange("p (m s) -> p m s", m=MT),
+                bump[h][:].rearrange("p (m s) -> p m s", m=MT),
                 seen_sb[:, h * SH : (h + 1) * SH].unsqueeze(1).to_broadcast([P, MT, SH]),
                 ALU.mult,
             )
-            lost = keep.tile([P, W], F32, name="lost%d" % h)
-            nc.vector.scalar_tensor_tensor(lost[:], surv[:], 1.0, alive[:], ALU.subtract, ALU.mult)
-            res = keep.tile([P, W], F32, name="res%d" % h)
+
+        def do_lost(h, cols):
             nc.vector.scalar_tensor_tensor(
-                res[:], lost[:], 1.0, hit[:].rearrange("p m s -> p (m s)"), ALU.add, ALU.subtract
+                lost[h][:, cols], surv[h][:, cols], 1.0, alive[h][:, cols], ALU.subtract, ALU.mult
             )
-            nc.sync.dma_start(
-                out[:, h * SH : (h + 1) * SH].rearrange("(m p) s -> p m s", p=P),
-                res[:].rearrange("p (m s) -> p m s", m=MT),
-            )
+
+        def do_res(h, cols):
+            nc.vector.scalar_tensor_tensor(res[h][:, cols], lost[h][:, cols], 1.0, hit[h][:, cols], ALU.add, ALU.subtract)
+
+        def store(h, m, queue):
+            queue.dma_start(out[m * P : (m + 1) * P, h * SH : (h + 1) * SH], res[h][:, m * SH : (m + 1) * SH])
+
+        whole = slice(0, W)
+        parts = [slice(m * SH, (m + 1) * SH) for m in range(MT)]
+        do_tanh(0)
+        do_ez(0)
+        do_bump(0)
+        do_surv(0, whole)
+        do_bump(1)
+        do_tanh(1)
+        do_ez(1)
+        do_surv(1, parts[0])
+        do_surv(1, parts[1])
+        do_alive(0)
+        do_hit(0)
+        do_lost(0, whole)
+        do_hit(1)
+        do_res(0, whole)
+        nc.sync.dma_start(
+            out[:, :SH].rearrange("(m p) s -> p m s", p=P), res[0][:].rearrange("p (m s) -> p m s", m=MT)
+        )
+        do_alive(1)
+        do_lost(1, parts[0])
+        do_lost(1, parts[1])
+        do_res(1, parts[0])
+        store(1, 0, nc.sync)
+        do_res(1, parts[1])
+        store(1, 1, nc.scalar)

@@ -37,13 +37,13 @@ def tile_picked_ywbaft_surv_p_kernel(tc, x_words, x_scales, w1, w2, w3, logt, se
         nc.sync.dma_start(offsets[:], offs)
         scale_table = keep.tile([P, T], U8, name="scale_table", tag="w2_codes", align_bytes=64)
         nc.vector.memset(scale_table[:].bitcast(I32), 0)
-        w2_raw = keep.tile([P, PACK, N], F32, name="w2_raw")
-        nc.sync.dma_start(w2_raw[:], rows_by_four(w2))
         for quad in range(4):
-            nc.sync.dma_start(
+            (nc.sync, nc.scalar)[quad % 2].dma_start(
                 scale_table[32 * quad : 32 * quad + 4, :].bitcast(I32),
                 x_scales[0, 4 * quad : 4 * quad + 4, :].bitcast(I32),
             )
+        w2_raw = keep.tile([P, PACK, N], F32, name="w2_raw")
+        nc.sync.dma_start(w2_raw[:], rows_by_four(w2))
         word_table = keep.tile([P, T], I32, name="word_table", align_bytes=64)
         nc.sync.dma_start(word_table[:], x_words[0].rearrange("p c t -> p (c t)").bitcast(I32))
         w1_raw = keep.tile([P, PACK, N], F32, name="w1_raw")
@@ -56,20 +56,18 @@ def tile_picked_ywbaft_surv_p_kernel(tc, x_words, x_scales, w1, w2, w3, logt, se
         nc.sync.dma_start(seen_sb[:], seen)
 
         eps = keep.tile([P, 1], F32, name="eps")
-        nc.gpsimd.memset(eps[:], EPS)
+        nc.vector.memset(eps[:], EPS)
         warm = keep.tile([P, 1], F32, name="warm")
         nc.scalar.activation(warm[:], eps[:], ACT.Sigmoid)
 
-        def interleave(raw, name, engines):
+        def interleave(raw, name, scalar_cols):
             grouped = keep.tile([P, N, PACK], BF16, name=name + "_bf", tag=name + "_bf", align_bytes=64)
-            for m in range(MT):
-                cols = slice(m * P, (m + 1) * P)
-                src = raw[:, :, cols].rearrange("p j (c i) -> p c j i", i=4)
-                dst = grouped[:, cols, :].rearrange("p (c i) j -> p c j i", i=4)
-                if engines[m] == "scalar":
-                    nc.scalar.copy(dst, src)
-                else:
-                    nc.vector.tensor_copy(dst, src)
+            for copy, cols in ((nc.scalar.copy, slice(0, scalar_cols)), (nc.vector.tensor_copy, slice(scalar_cols, N))):
+                if cols.stop > cols.start:
+                    copy(
+                        grouped[:, cols, :].rearrange("p (c i) j -> p c j i", i=4),
+                        raw[:, :, cols].rearrange("p j (c i) -> p c j i", i=4),
+                    )
             return grouped
 
         def quantize(grouped, name):
@@ -81,19 +79,12 @@ def tile_picked_ywbaft_surv_p_kernel(tc, x_words, x_scales, w1, w2, w3, logt, se
             return codes, scales
 
         x_code = []
-        x_scale = []
 
         def gather_words(h):
             xc = keep.tile([P, SH], U32, name="x_code%d" % h, tag=("x_code0", "w2_bf")[h], align_bytes=64)
             cols = SH // 16
             nc.vector.tensor_copy(xc[:], word_table[:].bitcast(U32).indirect(offsets[:, h * cols : (h + 1) * cols]))
             x_code.append(xc)
-
-        def gather_scales(h):
-            xs = keep.tile([P, SH], U8, name="x_scale%d" % h, align_bytes=64)
-            cols = SH // 16
-            nc.vector.tensor_copy(xs[:], scale_table[:].indirect(offsets[:, h * cols : (h + 1) * cols]))
-            x_scale.append(xs)
 
         def product(wq, h, name):
             codes, scales = wq
@@ -104,7 +95,7 @@ def tile_picked_ywbaft_surv_p_kernel(tc, x_words, x_scales, w1, w2, w3, logt, se
                     lhsT=codes[:, m * P : (m + 1) * P].bitcast(FP8X4),
                     lhsT_scale=scales[:, m * P : (m + 1) * P],
                     rhs=x_code[h][:].bitcast(FP8X4),
-                    rhs_scale=x_scale[h][:],
+                    rhs_scale=x_scale[:, h * SH : (h + 1) * SH],
                     start=True,
                     stop=True,
                 )
@@ -112,17 +103,17 @@ def tile_picked_ywbaft_surv_p_kernel(tc, x_words, x_scales, w1, w2, w3, logt, se
 
         sig = keep.tile([P, HALVES * W], F32, name="sig")
         ys = []
-        for h in range(HALVES):
-            gather_scales(h)
-        w2q = quantize(interleave(w2_raw, "w2", ("scalar", "scalar")), "w2")
+        x_scale = keep.tile([P, S], U8, name="x_scale", align_bytes=64)
+        nc.vector.tensor_copy(x_scale[:], scale_table[:].indirect(offsets[:]))
+        w2q = quantize(interleave(w2_raw, "w2", 160), "w2")
         for h in range(HALVES):
             gather_words(h)
             ys.append(product(w2q, h, "ys"))
             nc.scalar.activation(sig[:, h * W : (h + 1) * W], ys[h][:], ACT.Sigmoid, scale=-1.0)
 
-        w1q = quantize(interleave(w1_raw, "w1", ("vector", "vector")), "w1")
+        w1q = quantize(interleave(w1_raw, "w1", 0), "w1")
         ym = [product(w1q, h, "ym") for h in range(HALVES)]
-        w3q = quantize(interleave(w3_raw, "w3", ("vector", "vector")), "w3")
+        w3q = quantize(interleave(w3_raw, "w3", 0), "w3")
         yp = [product(w3q, h, "yp") for h in range(HALVES)]
         diff = []
         for h in range(HALVES):

from contextlib import ExitStack

import concourse.mybir as mybir

K, T, S, N = 512, 1024, 512, 256
FLOPS = 3 * 2 * K * N * S

F32 = mybir.dt.float32
BF16 = mybir.dt.bfloat16
I32 = mybir.dt.int32
U32 = mybir.dt.uint32
U16 = mybir.dt.uint16
U8 = mybir.dt.uint8
FP8X4 = mybir.dt.float8_e4m3fn_x4
ACT = mybir.ActivationFunctionType
ALU = mybir.AluOpType

P = 128
PACK = 4
MT = N // P
HALVES = 2
SH = S // HALVES
W = MT * SH
EPS = 2.0 ** -44


def tile_picked_ywbaft_surv_p_kernel(tc, x_words, x_scales, w1, w2, w3, logt, seen, offs, out):
    nc = tc.nc
    with ExitStack() as ctx:
        keep = ctx.enter_context(tc.tile_pool(name="keep", bufs=1))
        psum = ctx.enter_context(tc.psum_pool(name="psum", bufs=1))

        def rows_by_four(w):
            return w.rearrange("(p j) n -> p j n", j=PACK)

        offsets = keep.tile([P, S // 16], U16, name="offsets")
        nc.sync.dma_start(offsets[:], offs)
        scale_table = keep.tile([P, T], U8, name="scale_table", tag="w2_codes", align_bytes=64)
        nc.vector.memset(scale_table[:].bitcast(I32), 0)
        for quad in range(4):
            (nc.sync, nc.scalar)[quad % 2].dma_start(
                scale_table[32 * quad : 32 * quad + 4, :].bitcast(I32),
                x_scales[0, 4 * quad : 4 * quad + 4, :].bitcast(I32),
            )
        w2_raw = keep.tile([P, PACK, N], F32, name="w2_raw")
        nc.sync.dma_start(w2_raw[:], rows_by_four(w2))
        word_table = keep.tile([P, T], I32, name="word_table", align_bytes=64)
        nc.sync.dma_start(word_table[:], x_words[0].rearrange("p c t -> p (c t)").bitcast(I32))
        w1_raw = keep.tile([P, PACK, N], F32, name="w1_raw")
        nc.sync.dma_start(w1_raw[:], rows_by_four(w1))
        w3_raw = keep.tile([P, PACK, N], F32, name="w3_raw")
        nc.sync.dma_start(w3_raw[:], rows_by_four(w3))
        logt_sb = keep.tile([P, MT, S], F32, name="logt_sb")
        nc.sync.dma_start(logt_sb[:], logt.rearrange("(m p) s -> p m s", p=P))
        seen_sb = keep.tile([P, S], F32, name="seen_sb")
        nc.sync.dma_start(seen_sb[:], seen)

        eps = keep.tile([P, 1], F32, name="eps")
        nc.vector.memset(eps[:], EPS)
        warm = keep.tile([P, 1], F32, name="warm")
        nc.scalar.activation(warm[:], eps[:], ACT.Sigmoid)

        def interleave(raw, name, scalar_cols):
            grouped = keep.tile([P, N, PACK], BF16, name=name + "_bf", tag=name + "_bf", align_bytes=64)
            for copy, cols in ((nc.scalar.copy, slice(0, scalar_cols)), (nc.vector.tensor_copy, slice(scalar_cols, N))):
                if cols.stop > cols.start:
                    copy(
                        grouped[:, cols, :].rearrange("p (c i) j -> p c j i", i=4),
                        raw[:, :, cols].rearrange("p j (c i) -> p c j i", i=4),
                    )
            return grouped

        def quantize(grouped, name):
            codes = keep.tile([P, N], U32, name=name + "_codes", tag=name + "_codes", align_bytes=64)
            scales = keep.tile([P, N], U8, name=name + "_scales", align_bytes=64)
            nc.vector.quantize_mx(
                out=codes[:].bitcast(FP8X4), scales=scales[:], in_=grouped[:].rearrange("p n j -> p (n j)")
            )
            return codes, scales

        x_code = []

        def gather_words(h):
            xc = keep.tile([P, SH], U32, name="x_code%d" % h, tag=("x_code0", "w2_bf")[h], align_bytes=64)
            cols = SH // 16
            nc.vector.tensor_copy(xc[:], word_table[:].bitcast(U32).indirect(offsets[:, h * cols : (h + 1) * cols]))
            x_code.append(xc)

        def product(wq, h, name):
            codes, scales = wq
            bank = psum.tile([P, W], F32, name="%s%d" % (name, h))
            for m in range(MT):
                nc.tensor.matmul_mx(
                    out=bank[:, m * SH : (m + 1) * SH],
                    lhsT=codes[:, m * P : (m + 1) * P].bitcast(FP8X4),
                    lhsT_scale=scales[:, m * P : (m + 1) * P],
                    rhs=x_code[h][:].bitcast(FP8X4),
                    rhs_scale=x_scale[:, h * SH : (h + 1) * SH],
                    start=True,
                    stop=True,
                )
            return bank

        sig = keep.tile([P, HALVES * W], F32, name="sig")
        ys = []
        x_scale = keep.tile([P, S], U8, name="x_scale", align_bytes=64)
        nc.vector.tensor_copy(x_scale[:], scale_table[:].indirect(offsets[:]))
        w2q = quantize(interleave(w2_raw, "w2", 160), "w2")
        for h in range(HALVES):
            gather_words(h)
            ys.append(product(w2q, h, "ys"))
            nc.scalar.activation(sig[:, h * W : (h + 1) * W], ys[h][:], ACT.Sigmoid, scale=-1.0)

        w1q = quantize(interleave(w1_raw, "w1", 0), "w1")
        ym = [product(w1q, h, "ym") for h in range(HALVES)]
        w3q = quantize(interleave(w3_raw, "w3", 0), "w3")
        yp = [product(w3q, h, "yp") for h in range(HALVES)]
        diff = []
        for h in range(HALVES):
            d = keep.tile([P, W], F32, name="diff%d" % h)
            nc.vector.tensor_tensor(
                d[:].rearrange("p (m s) -> p m s", m=MT),
                ym[h][:].rearrange("p (m s) -> p m s", m=MT),
                logt_sb[:, :, h * SH : (h + 1) * SH],
                ALU.subtract,
            )
            diff.append(d)

        lg = keep.tile([P, HALVES * W], F32, name="lg")
        nc.scalar.activation(lg[:, : W + 8], sig[:, : W + 8], ACT.Ln, bias=eps[:])
        nc.scalar.activation(lg[:, W + 8 :], sig[:, W + 8 :], ACT.Ln, bias=eps[:])

        neg = []
        for h in range(HALVES):
            ng = keep.tile([P, W], F32, name="neg%d" % h, tag=("w3_bf", "w1_bf")[h], align_bytes=64)
            nc.vector.scalar_tensor_tensor(ng[:], ys[h][:], -1.0, lg[:, h * W : (h + 1) * W], ALU.mult, ALU.min)
            neg.append(ng)
        z = []
        for h in range(HALVES):
            zz = keep.tile([P, W], F32, name="z%d" % h)
            nc.vector.scalar_tensor_tensor(zz[:], neg[h][:], 0.4, diff[h][:], ALU.subtract, ALU.mult)
            z.append(zz)
        zsq = []
        for h in range(HALVES):
            q = keep.tile([P, W], F32, name="zsq%d" % h)
            nc.vector.tensor_tensor(q[:], z[h][:], z[h][:], ALU.mult)
            zsq.append(q)
        th = [sig[:, (1 - h) * W : (2 - h) * W] for h in range(HALVES)]
        bump = [keep.tile([P, W], F32, name="bump%d" % h) for h in range(HALVES)]
        ez = [keep.tile([P, W], F32, name="ez%d" % h) for h in range(HALVES)]
        surv = [keep.tile([P, W], F32, name="surv%d" % h) for h in range(HALVES)]
        alive = [keep.tile([P, W], F32, name="alive%d" % h) for h in range(HALVES)]
        hit = [keep.tile([P, W], F32, name="hit%d" % h) for h in range(HALVES)]
        lost = [keep.tile([P, W], F32, name="lost%d" % h) for h in range(HALVES)]
        res = [keep.tile([P, W], F32, name="res%d" % h) for h in range(HALVES)]

        def do_tanh(h):
            nc.scalar.activation(th[h], yp[h][:], ACT.Tanh, scale=0.5)

        def do_ez(h):
            nc.scalar.activation(ez[h][:], z[h][:], ACT.Exp, scale=0.6)

        def do_bump(h):
            nc.scalar.activation(bump[h][:], zsq[h][:], ACT.Exp, scale=-0.36)

        def do_surv(h, cols):
            nc.scalar.activation(surv[h][:, cols], ez[h][:, cols], ACT.Exp, scale=-1.0)

        def do_alive(h):
            nc.vector.tensor_scalar(alive[h][:], th[h], -0.3, 0.7, ALU.mult, ALU.add)

        def do_hit(h):
            nc.vector.tensor_tensor(
                hit[h][:].rearrange("p (m s) -> p m s", m=MT),
                bump[h][:].rearrange("p (m s) -> p m s", m=MT),
                seen_sb[:, h * SH : (h + 1) * SH].unsqueeze(1).to_broadcast([P, MT, SH]),
                ALU.mult,
            )

        def do_lost(h, cols):
            nc.vector.scalar_tensor_tensor(
                lost[h][:, cols], surv[h][:, cols], 1.0, alive[h][:, cols], ALU.subtract, ALU.mult
            )

        def do_res(h, cols):
            nc.vector.scalar_tensor_tensor(res[h][:, cols], lost[h][:, cols], 1.0, hit[h][:, cols], ALU.add, ALU.subtract)

        def store(h, m, queue):
            queue.dma_start(out[m * P : (m + 1) * P, h * SH : (h + 1) * SH], res[h][:, m * SH : (m + 1) * SH])

        whole = slice(0, W)
        parts = [slice(m * SH, (m + 1) * SH) for m in range(MT)]
        do_tanh(0)
        do_ez(0)
        do_bump(0)
        do_surv(0, whole)
        do_bump(1)
        do_tanh(1)
        do_ez(1)
        do_surv(1, parts[0])
        do_surv(1, parts[1])
        do_alive(0)
        do_hit(0)
        do_lost(0, whole)
        do_hit(1)
        do_res(0, whole)
        nc.sync.dma_start(
            out[:, :SH].rearrange("(m p) s -> p m s", p=P), res[0][:].rearrange("p (m s) -> p m s", m=MT)
        )
        do_alive(1)
        do_lost(1, parts[0])
        do_lost(1, parts[1])
        do_res(1, parts[0])
        store(1, 0, nc.sync)
        do_res(1, parts[1])
        store(1, 1, nc.scalar)
